import numpy as np
import ml_dtypes


def mxq(x, axis, fmt="e4m3"):
    dtype, down = {"e4m3": (ml_dtypes.float8_e4m3fn, 7), "e5m2": (ml_dtypes.float8_e5m2, 14)}[fmt]
    v = np.moveaxis(np.asarray(x, np.float32).astype(ml_dtypes.bfloat16).astype(np.float64), axis, -1)
    blocks = v.reshape(v.shape[:-1] + (-1, 32))
    amax = np.abs(blocks).max(-1, keepdims=True)
    byte = np.maximum(np.where(amax > 0, np.frexp(amax)[1] - 1 + 127, 0) - down, 1)
    scale = np.exp2(byte - 127.0)
    codes = (blocks / scale).astype(np.float32).astype(dtype).astype(np.float64)
    return np.moveaxis((codes * scale).reshape(v.shape), -1, axis)


WIDE = False


def mx_kscale(k):
    if not WIDE:
        return np.ones(k)
    levels = np.array([10, -10, 5, -5, 0])
    if k % 512:
        return np.exp2(np.random.permutation(np.resize(levels, k // 32))).repeat(32)
    a = np.empty((k // 512, 16))
    for p in range(k // 512):
        a[p, :8] = np.random.permutation(np.resize(levels, 8))
        for g in range(8):
            far = levels[np.abs(levels - a[p, g]) >= 10]
            a[p, g + 8] = far[np.random.randint(len(far))]
    return np.exp2(a.ravel()).repeat(32)


def f64(x):
    return np.asarray(x).astype(np.float64)


def striped(idx):
    return np.tile(idx.reshape(-1, 16).T, (8, 1)).astype(np.uint16)


def unstriped(offs):
    return offs[:16].T.reshape(-1).astype(np.int64)


E2M1 = np.array([0.0, 0.5, 1.0, 1.5, 2.0, 3.0, 4.0, 6.0, -0.0, -0.5, -1.0, -1.5, -2.0, -3.0, -4.0, -6.0])


def pack_weight(w, fmt):
    k, n = w.shape
    w = f64(np.asarray(w, np.float32).astype(ml_dtypes.bfloat16)).reshape(k // 32, 32, n)
    amax = np.abs(w).max(1)
    if fmt == "e4m3":
        byte = np.frexp(amax)[1] - 1 + 127 - 7
    else:
        mant, ex = np.frexp(amax / 6.0)
        byte = np.where(mant > 0.5, ex, ex - 1) + 127
    byte = np.clip(np.where(amax > 0, byte, 1), 1, 254)
    scaled = (w * np.exp2(127.0 - byte)[:, None, :]).reshape(k, n).astype(np.float32)
    by_word = np.ascontiguousarray(scaled.reshape(k // 512, 128, 4, n).transpose(0, 1, 3, 2))
    if fmt == "e4m3":
        words = by_word.astype(ml_dtypes.float8_e4m3fn).view(np.uint8)
    else:
        c = by_word.astype(ml_dtypes.float4_e2m1fn).view(np.uint8) & 0xF
        words = (c[..., 0::2] | (c[..., 1::2] << 4)).reshape(k // 512, 128, 2 * n)
    return np.ascontiguousarray(words), np.ascontiguousarray(byte.astype(np.uint8).reshape(k // 512, 16, n))


def unpack_weight(words, scales, fmt):
    g, _, n = scales.shape
    words = np.ascontiguousarray(words).reshape(g, 128, n, -1)
    if fmt == "e4m3":
        vals = words.view(ml_dtypes.float8_e4m3fn).astype(np.float64)
    else:
        nib = np.empty((g, 128, n, 4), np.uint8)
        nib[..., 0::2] = words & 0xF
        nib[..., 1::2] = words >> 4
        vals = E2M1[nib]
    vals = vals * np.repeat(np.exp2(scales.astype(np.float64) - 127.0), 8, axis=1)[..., None]
    return vals.transpose(0, 1, 3, 2).reshape(g * 512, n)


def gelu(v):
    return 0.5 * v * (1.0 + np.tanh(np.sqrt(2.0 / np.pi) * (v + 0.044715 * v**3)))


K, T, S, H, T2, P, N = 1024, 2048, 1024, 512, 2048, 512, 384


def setup_inputs():
    n = np.random.standard_normal
    s = mx_kscale(K)[:, None]
    u = mx_kscale(H)[:, None]
    tab_words, tab_scales = pack_weight(n((K, T)) * s, "e4m3")
    w1 = (n((K, H)) / np.sqrt(K) / s * u.T).astype(np.float32)
    w2_words, w2_scales = pack_weight(0.55 * n((K, H)) / np.sqrt(K) / s, "e2m1")
    shift = (0.7 * n(H) * u[:, 0]).astype(np.float32)
    wgs = np.exp(0.3 * n((128, S))).astype(np.float32)
    page0 = (n((H, T2)) * u).astype(np.float32)
    terms = (0.8 * n((H, P)) * u).astype(np.float32)
    w3 = (n((H, N)) / np.sqrt(H) / u).astype(np.float32)
    w4_words, w4_scales = pack_weight(n((H, N)) / np.sqrt(H) / u, "e4m3")
    perm = np.random.permutation(T2)
    return {"tab_words": tab_words, "tab_scales": tab_scales, "offs": striped(np.random.permutation(T)[:S]),
            "offs2": striped(np.random.permutation(T2)[:S]), "offs3": striped(perm[:P]), "offs4": striped(perm[P:2 * P]),
            "w1": w1, "w2_words": w2_words, "w2_scales": w2_scales, "shift": shift, "wgs": wgs, "page0": page0,
            "terms": terms, "w3": w3, "w4_words": w4_words, "w4_scales": w4_scales}


def reference(tab_words, tab_scales, offs, offs2, offs3, offs4, w1, w2_words, w2_scales, shift, wgs, page0, terms, w3, w4_words, w4_scales):
    v = unpack_weight(tab_words, tab_scales, "e4m3")[:, unstriped(offs)]
    w2 = unpack_weight(w2_words, w2_scales, "e2m1")
    w4 = unpack_weight(w4_words, w4_scales, "e4m3")
    d1 = mxq(f64(w1), 0, "e4m3").T @ v
    d2 = w2.T @ v
    h = d1 * np.cos(d2) + f64(shift)[:, None]
    page = f64(page0).copy()
    page[:, unstriped(offs2)] = np.tile(f64(wgs), (H // 128, 1)) * h
    a = page[:, unstriped(offs3)]
    b = page[:, unstriped(offs4)]
    page[:, unstriped(offs3)] = np.maximum(a, b + f64(terms))
    page[:, unstriped(offs4)] = np.minimum(a, b)
    pq = mxq(page, 0, "e4m3")
    e1 = mxq(f64(w3), 0, "e4m3").T @ pq
    e2 = w4.T @ pq
    return np.maximum(e1, e2)

@@ -1,0 +1,300 @@
+from contextlib import ExitStack
+
+import concourse.mybir as mybir
+
+K, T, S, H, T2, NPAIR, N = 1024, 2048, 1024, 512, 2048, 512, 384
+FLOPS = 2 * 2 * K * H * S + 2 * 2 * H * N * T2
+
+F32 = mybir.dt.float32
+BF16 = mybir.dt.bfloat16
+I32 = mybir.dt.int32
+U32 = mybir.dt.uint32
+U16 = mybir.dt.uint16
+U8 = mybir.dt.uint8
+FP8X4 = mybir.dt.float8_e4m3fn_x4
+FP4X4 = mybir.dt.float4_e2m1fn_x4
+ALU = mybir.AluOpType
+ACT = mybir.ActivationFunctionType
+
+P = 128
+PACK = 4
+PASSES = K // (P * PACK)
+BANK = 512
+HALVES = S // BANK
+CHUNKS = T2 // BANK
+NT = N // P
+QUADS = 4
+ORDER = (0, 2, 3, 1)
+VECTOR_CHUNKS = 2
+
+
+def tile_list_slot_trade_table_kernel(
+    tc, tab_words, tab_scales, offs, offs2, offs3, offs4, w1, w2_words, w2_scales,
+    shift, wgs, page0, terms, w3, w4_words, w4_scales, out,
+):
+    nc = tc.nc
+    with ExitStack() as ctx:
+        keep = ctx.enter_context(tc.tile_pool(name="keep", bufs=1))
+        ring = ctx.enter_context(tc.tile_pool(name="ring", bufs=2))
+        psum = ctx.enter_context(tc.psum_pool(name="psum", bufs=4))
+
+        def held(shape, dtype, name):
+            return keep.tile(shape, dtype, name=name, align_bytes=64)
+
+        idx = held([P, S // 16], U16, "idx")
+        idx2 = held([P, S // 16], U16, "idx2")
+        idx3 = held([P, NPAIR // 16], U16, "idx3")
+        idx4 = held([P, NPAIR // 16], U16, "idx4")
+
+        tab_sc = held([P, T], U8, "tab_sc")
+        v_sc1 = held([P, S], U8, "v_sc1")
+        w2_sc_raw = held([P, PASSES, H], U8, "w2_sc_raw")
+        w4_sc = held([P, N], U8, "w4_sc")
+        nc.vector.memset(tab_sc[:].bitcast(I32), 0)
+        nc.vector.memset(v_sc1[:].bitcast(I32), 0)
+        nc.gpsimd.memset(w2_sc_raw[:].rearrange("p a c -> p (a c)").bitcast(I32), 0)
+        nc.gpsimd.memset(w4_sc[:].bitcast(I32), 0)
+
+        nc.sync.dma_start(idx[:], offs)
+        for q in range(QUADS):
+            nc.scalar.dma_start(
+                tab_sc[32 * q : 32 * q + 8, :].bitcast(I32),
+                tab_scales[:, 4 * q : 4 * q + 4, :].bitcast(I32),
+            )
+        for q in range(QUADS):
+            nc.gpsimd.dma_start(
+                w2_sc_raw[32 * q : 32 * q + 4, :, :].bitcast(I32),
+                w2_scales[:, 4 * q : 4 * q + 4, :].rearrange("a r c -> r a c").bitcast(I32),
+            )
+        shift_sb = held([P, PACK], F32, "shift_sb")
+        nc.gpsimd.dma_start(shift_sb[:], shift.rearrange("(p t) -> p t", t=PACK))
+
+        tab_w = [held([P, T], U32, "tab_w%d" % a) for a in range(PASSES)]
+        for a in range(PASSES):
+            nc.sync.dma_start(
+                tab_w[a][:].bitcast(I32),
+                tab_words[a].rearrange("p t i -> p (t i)").bitcast(I32),
+            )
+        w2_raw = held([P, PASSES, 2 * H], U8, "w2_raw")
+        nc.sync.dma_start(
+            w2_raw[:].bitcast(I32), w2_words.rearrange("a p c -> p a c").bitcast(I32)
+        )
+        w1_raw = [held([P, PACK, H], F32, "w1_raw%d" % a) for a in range(PASSES)]
+        for a in range(PASSES):
+            nc.sync.dma_start(
+                w1_raw[a][:],
+                w1[512 * a : 512 * (a + 1), :].rearrange("(p j) c -> p j c", j=PACK),
+            )
+
+        wgs_rows = wgs.rearrange("(q t) j -> q t j", t=PACK)
+        wg_first = held([P, S], F32, "wg_first")
+        for q in range(QUADS):
+            nc.sync.dma_start(wg_first[32 * q : 32 * q + 32, :], wgs_rows[:, 0, :])
+        page_rows = page0.rearrange("(p t) c -> p t c", t=PACK)
+        terms_rows = terms.rearrange("(p t) m -> p t m", t=PACK)
+        page = [held([P, T2], F32, "page%d" % t) for t in range(PACK)]
+        term = [held([P, NPAIR], F32, "term%d" % t) for t in range(PACK)]
+        nc.sync.dma_start(page[0][:], page_rows[:, 0, :])
+        nc.sync.dma_start(idx2[:], offs2)
+        nc.sync.dma_start(idx4[:], offs4)
+        nc.sync.dma_start(idx3[:], offs3)
+        nc.sync.dma_start(term[0][:], terms_rows[:, 0, :])
+        wg_rest = held([P, PACK - 1, S], F32, "wg_rest")
+        for q in range(QUADS):
+            nc.sync.dma_start(wg_rest[32 * q : 32 * q + 32, :, :], wgs_rows[:, 1:, :])
+        for t in ORDER[1:]:
+            nc.sync.dma_start(page[t][:], page_rows[:, t, :])
+            nc.sync.dma_start(term[t][:], terms_rows[:, t, :])
+        w3_raw = held([P, PACK, N], F32, "w3_raw")
+        nc.sync.dma_start(w3_raw[:], w3.rearrange("(p j) c -> p j c", j=PACK))
+        w4_w = held([P, N], U32, "w4_w")
+        nc.sync.dma_start(
+            w4_w[:].bitcast(I32), w4_words[0].rearrange("p c i -> p (c i)").bitcast(I32)
+        )
+        for q in range(QUADS):
+            nc.sync.dma_start(
+                w4_sc[32 * q : 32 * q + 4, :].bitcast(I32),
+                w4_scales[0, 4 * q : 4 * q + 4, :].bitcast(I32),
+            )
+
+        def wg(t):
+            return wg_first[:] if t == 0 else wg_rest[:, t - 1, :]
+
+        v_sc0 = held([P, S], U8, "v_sc0")
+        nc.vector.tensor_copy(v_sc0[:], tab_sc[:].indirect(idx[:]))
+        nc.scalar.dma_start(v_sc1[0:112, :].bitcast(I32), v_sc0[4:116, :].bitcast(I32))
+        v_sc = [v_sc0, v_sc1]
+        v_w = [[held([P, BANK], U32, "v_w%d_%d" % (a, u)) for u in range(HALVES)] for a in range(PASSES)]
+
+        def gather_words(a, u):
+            nc.vector.tensor_copy(
+                v_w[a][u][:], tab_w[a][:].indirect(idx[:, 32 * u : 32 * (u + 1)])
+            )
+
+        w2_sc = held([P, PASSES, H], U8, "w2_sc")
+        w2_w = held([P, PASSES, 2 * H], U8, "w2_w")
+        gather_words(0, 0)
+        nc.vector.tensor_copy(
+            w2_sc[:].rearrange("p a (t m) -> p a m t", t=PACK),
+            w2_sc_raw[:].rearrange("p a (m t) -> p a m t", t=PACK),
+        )
+        gather_words(0, 1)
+        gather_words(1, 0)
+        gather_words(1, 1)
+        nc.scalar.copy(
+            w2_w[:].bitcast(U16).rearrange("p a (t m) -> p a m t", t=PACK),
+            w2_raw[:].bitcast(U16).rearrange("p a (m t) -> p a m t", t=PACK),
+        )
+
+        w1_bf0 = held([P, PACK, P, PACK], BF16, "w1_bf0")
+        w1_c0 = held([P, H], U32, "w1_c0")
+        w1_s0 = held([P, H], U8, "w1_s0")
+        nc.scalar.copy(
+            w1_bf0[:].rearrange("p t m j -> p m j t"),
+            w1_raw[0][:].rearrange("p j (m t) -> p m j t", t=PACK),
+        )
+        nc.vector.quantize_mx(
+            w1_c0[:].bitcast(FP8X4), w1_s0[:], w1_bf0[:].rearrange("p t m j -> p (t m j)")
+        )
+        w1_bf1a = held([P, P, PACK], BF16, "w1_bf1a")
+        w1_c1a = held([P, P], U32, "w1_c1a")
+        w1_s1a = held([P, P], U8, "w1_s1a")
+        w1_bf1b = held([P, PACK - 1, P, PACK], BF16, "w1_bf1b")
+        w1_c1b = held([P, (PACK - 1) * P], U32, "w1_c1b")
+        w1_s1b = held([P, (PACK - 1) * P], U8, "w1_s1b")
+        w1_cols = w1_raw[1][:].rearrange("p j (m t) -> p m j t", t=PACK)
+        nc.vector.tensor_copy(w1_bf1a[:], w1_cols[:, :, :, 0])
+        nc.vector.quantize_mx(
+            w1_c1a[:].bitcast(FP8X4), w1_s1a[:], w1_bf1a[:].rearrange("p m j -> p (m j)")
+        )
+
+        def w1_rest():
+            nc.scalar.copy(w1_bf1b[:].rearrange("p t m j -> p m j t"), w1_cols[:, :, :, 1:])
+            nc.vector.quantize_mx(
+                w1_c1b[:].bitcast(FP8X4), w1_s1b[:], w1_bf1b[:].rearrange("p t m j -> p (t m j)")
+            )
+
+        def w1_operand(a, t):
+            if a == 0:
+                return w1_c0[:, P * t : P * (t + 1)], w1_s0[:, P * t : P * (t + 1)]
+            if t == 0:
+                return w1_c1a[:], w1_s1a[:]
+            return w1_c1b[:, P * (t - 1) : P * t], w1_s1b[:, P * (t - 1) : P * t]
+
+        def phases(t, u):
+            d2 = psum.tile([P, BANK], F32, name="scalar_bank")
+            for a in range(PASSES):
+                nc.tensor.matmul_mx(
+                    d2[:],
+                    lhsT=w2_w[:, a, 2 * P * t : 2 * P * (t + 1)].bitcast(FP4X4),
+                    lhsT_scale=w2_sc[:, a, P * t : P * (t + 1)],
+                    rhs=v_w[a][u][:].bitcast(FP8X4),
+                    rhs_scale=v_sc[a][:, BANK * u : BANK * (u + 1)],
+                    start=(a == 0),
+                    stop=(a == PASSES - 1),
+                )
+            sin_half = ring.tile([P, BANK], F32, name="sin_half")
+            nc.scalar.activation(sin_half[:], d2[:], ACT.Sin, scale=0.5)
+            sq = ring.tile([P, BANK], F32, name="sq", bufs=4)
+            nc.scalar.activation(sq[:], sin_half[:], ACT.Square)
+            return sq
+
+        def features(t, u, sq, h):
+            d1 = psum.tile([P, BANK], F32, name="vector_bank")
+            for a in range(PASSES):
+                codes, scales = w1_operand(a, t)
+                nc.tensor.matmul_mx(
+                    d1[:],
+                    lhsT=codes.bitcast(FP8X4),
+                    lhsT_scale=scales,
+                    rhs=v_w[a][u][:].bitcast(FP8X4),
+                    rhs_scale=v_sc[a][:, BANK * u : BANK * (u + 1)],
+                    start=(a == 0),
+                    stop=(a == PASSES - 1),
+                )
+            prod = ring.tile([P, BANK], F32, name="prod")
+            nc.vector.scalar_tensor_tensor(prod[:], sq[:], -0.5, d1[:], ALU.add, ALU.mult)
+            nc.scalar.activation(
+                h[:, BANK * u : BANK * (u + 1)], prod[:], ACT.Identity,
+                bias=shift_sb[:, t : t + 1], scale=-2.0,
+            )
+
+        page_bf = [held([P, BANK, PACK], BF16, "page_bf%d" % c) for c in range(CHUNKS)]
+
+        def round_page(t, c, engine_copy):
+            engine_copy(page_bf[c][:, :, t], page[t][:, BANK * c : BANK * (c + 1)])
+
+        t0 = ORDER[0]
+        h = ring.tile([P, S], F32, name="h")
+        sqs = [phases(t0, u) for u in range(HALVES)]
+        for u in range(HALVES):
+            features(t0, u, sqs[u], h)
+        w1_rest()
+
+        w3_bf = held([P, N, PACK], BF16, "w3_bf")
+        w3_c = held([P, N], U32, "w3_c")
+        w3_s = held([P, N], U8, "w3_s")
+
+        for step, t in enumerate(ORDER):
+            nxt = ORDER[step + 1] if step + 1 < PACK else None
+            nc.vector.tensor_tensor(page[t][:].indirect(idx2[:]), h[:], wg(t), ALU.mult)
+            if nxt is not None:
+                h = ring.tile([P, S], F32, name="h")
+                sqs = [phases(nxt, u) for u in range(HALVES)]
+                features(nxt, 0, sqs[0], h)
+            else:
+                nc.scalar.copy(
+                    w3_bf[:].rearrange("p (c i) j -> p c j i", i=4),
+                    w3_raw[:].rearrange("p j (c i) -> p c j i", i=4),
+                )
+                nc.vector.quantize_mx(
+                    w3_c[:].bitcast(FP8X4), w3_s[:], w3_bf[:].rearrange("p c j -> p (c j)")
+                )
+            evening = ring.tile([P, NPAIR], F32, name="evening")
+            morning = ring.tile([P, NPAIR], F32, name="morning")
+            traded = ring.tile([P, NPAIR], F32, name="traded")
+            low = ring.tile([P, NPAIR], F32, name="low")
+            high = ring.tile([P, NPAIR], F32, name="high")
+            nc.vector.tensor_copy(evening[:], page[t][:].indirect(idx4[:]))
+            nc.vector.tensor_copy(morning[:], page[t][:].indirect(idx3[:]))
+            nc.vector.tensor_tensor(traded[:], evening[:], term[t][:], ALU.add)
+            nc.vector.tensor_tensor(low[:], morning[:], evening[:], ALU.min)
+            nc.vector.tensor_tensor(high[:], morning[:], traded[:], ALU.max)
+            nc.vector.tensor_copy(page[t][:].indirect(idx4[:]), low[:])
+            if nxt is not None:
+                features(nxt, 1, sqs[1], h)
+            nc.vector.tensor_copy(page[t][:].indirect(idx3[:]), high[:])
+            if nxt is not None:
+                for c in range(CHUNKS):
+                    round_page(t, c, nc.scalar.copy)
+
+        last = ORDER[-1]
+        for c in range(CHUNKS):
+            round_page(last, c, nc.vector.tensor_copy if c < VECTOR_CHUNKS else nc.scalar.copy)
+        page_c = [held([P, BANK], U32, "page_c%d" % c) for c in range(CHUNKS)]
+        page_s = [held([P, BANK], U8, "page_s%d" % c) for c in range(CHUNKS)]
+        for c in range(CHUNKS):
+            nc.vector.quantize_mx(
+                page_c[c][:].bitcast(FP8X4), page_s[c][:],
+                page_bf[c][:].rearrange("p c j -> p (c j)"),
+            )
+        for c in range(CHUNKS):
+            for n in range(NT):
+                cols = slice(P * n, P * (n + 1))
+                e1 = psum.tile([P, BANK], F32, name="scalar_bank")
+                e2 = psum.tile([P, BANK], F32, name="vector_bank")
+                for acc, codes, scales in ((e1, w3_c, w3_s), (e2, w4_w, w4_sc)):
+                    nc.tensor.matmul_mx(
+                        acc[:],
+                        lhsT=codes[:, cols].bitcast(FP8X4),
+                        lhsT_scale=scales[:, cols],
+                        rhs=page_c[c][:].bitcast(FP8X4),
+                        rhs_scale=page_s[c][:],
+                        start=True,
+                        stop=True,
+                    )
+                first = ring.tile([P, BANK], F32, name="first", bufs=3)
+                nc.scalar.copy(first[:], e1[:])
+                best = ring.tile([P, BANK], F32, name="best", bufs=6)
+                nc.vector.tensor_tensor(best[:], e2[:], first[:], ALU.max)
+                nc.sync.dma_start(out[cols, BANK * c : BANK * (c + 1)], best[:])

@@ -46,56 +46,70 @@ def tile_list_slot_trade_table_kernel(
         idx3 = held([P, NPAIR // 16], U16, "idx3")
         idx4 = held([P, NPAIR // 16], U16, "idx4")
 
-        tab_sc = held([P, T], U8, "tab_sc")
-        v_sc1 = held([P, S], U8, "v_sc1")
+        tab_sc = held([P, PASSES, T], U8, "tab_sc")
         w2_sc_raw = held([P, PASSES, H], U8, "w2_sc_raw")
         w4_sc = held([P, N], U8, "w4_sc")
-        nc.vector.memset(tab_sc[:].bitcast(I32), 0)
-        nc.vector.memset(v_sc1[:].bitcast(I32), 0)
+        nc.gpsimd.memset(tab_sc[:, 0, :].bitcast(I32), 0)
+        nc.vector.memset(tab_sc[:, 1, :].bitcast(I32), 0)
         nc.gpsimd.memset(w2_sc_raw[:].rearrange("p a c -> p (a c)").bitcast(I32), 0)
-        nc.gpsimd.memset(w4_sc[:].bitcast(I32), 0)
-
-        nc.sync.dma_start(idx[:], offs)
-        for q in range(QUADS):
-            nc.scalar.dma_start(
-                tab_sc[32 * q : 32 * q + 8, :].bitcast(I32),
-                tab_scales[:, 4 * q : 4 * q + 4, :].bitcast(I32),
-            )
-        for q in range(QUADS):
-            nc.gpsimd.dma_start(
-                w2_sc_raw[32 * q : 32 * q + 4, :, :].bitcast(I32),
-                w2_scales[:, 4 * q : 4 * q + 4, :].rearrange("a r c -> r a c").bitcast(I32),
-            )
-        shift_sb = held([P, PACK], F32, "shift_sb")
-        nc.gpsimd.dma_start(shift_sb[:], shift.rearrange("(p t) -> p t", t=PACK))
+        nc.vector.memset(w4_sc[:].bitcast(I32), 0)
 
         tab_w = [held([P, T], U32, "tab_w%d" % a) for a in range(PASSES)]
-        for a in range(PASSES):
+        w1_raw = [held([P, PACK, H], F32, "w1_raw%d" % a) for a in range(PASSES)]
+
+        def load_words(a):
             nc.sync.dma_start(
                 tab_w[a][:].bitcast(I32),
                 tab_words[a].rearrange("p t i -> p (t i)").bitcast(I32),
             )
-        w2_raw = held([P, PASSES, 2 * H], U8, "w2_raw")
-        nc.sync.dma_start(
-            w2_raw[:].bitcast(I32), w2_words.rearrange("a p c -> p a c").bitcast(I32)
-        )
-        w1_raw = [held([P, PACK, H], F32, "w1_raw%d" % a) for a in range(PASSES)]
-        for a in range(PASSES):
+
+        def load_w1(a):
             nc.sync.dma_start(
                 w1_raw[a][:],
                 w1[512 * a : 512 * (a + 1), :].rearrange("(p j) c -> p j c", j=PACK),
             )
 
-        wgs_rows = wgs.rearrange("(q t) j -> q t j", t=PACK)
-        wg_first = held([P, S], F32, "wg_first")
+        w2_raw = held([P, PASSES, 2 * H], U8, "w2_raw")
+        nc.sync.dma_start(
+            w2_raw[:].bitcast(I32), w2_words.rearrange("a p c -> p a c").bitcast(I32)
+        )
         for q in range(QUADS):
-            nc.sync.dma_start(wg_first[32 * q : 32 * q + 32, :], wgs_rows[:, 0, :])
+            nc.sync.dma_start(
+                tab_sc[32 * q : 32 * q + 4, :, :].bitcast(I32),
+                tab_scales[:, 4 * q : 4 * q + 4, :].rearrange("a r t -> r a t").bitcast(I32),
+            )
+        nc.sync.dma_start(idx[:], offs)
+        load_words(0)
+        load_words(1)
+        for q in range(QUADS):
+            nc.sync.dma_start(
+                w2_sc_raw[32 * q : 32 * q + 4, :, :].bitcast(I32),
+                w2_scales[:, 4 * q : 4 * q + 4, :].rearrange("a r c -> r a c").bitcast(I32),
+            )
+        load_w1(0)
+        load_w1(1)
+        shift_sb = held([P, PACK], F32, "shift_sb")
+        nc.sync.dma_start(shift_sb[:], shift.rearrange("(p t) -> p t", t=PACK))
+
+        wgs_rows = wgs.rearrange("(q t) j -> q t j", t=PACK)
+        wg_first = [
+            keep.tile([P, BANK], F32, name="wg_first%d" % u, tag="wg_first%d" % u, align_bytes=64)
+            for u in range(HALVES)
+        ]
+
+        def load_wg_first(u):
+            cols = slice(BANK * u, BANK * (u + 1))
+            for q in range(QUADS):
+                nc.sync.dma_start(wg_first[u][32 * q : 32 * q + 32, :], wgs_rows[:, 0, cols])
+
+        nc.sync.dma_start(idx2[:], offs2)
+        load_wg_first(0)
         page_rows = page0.rearrange("(p t) c -> p t c", t=PACK)
         terms_rows = terms.rearrange("(p t) m -> p t m", t=PACK)
         page = [held([P, T2], F32, "page%d" % t) for t in range(PACK)]
         term = [held([P, NPAIR], F32, "term%d" % t) for t in range(PACK)]
         nc.sync.dma_start(page[0][:], page_rows[:, 0, :])
-        nc.sync.dma_start(idx2[:], offs2)
+        load_wg_first(1)
         nc.sync.dma_start(idx4[:], offs4)
         nc.sync.dma_start(idx3[:], offs3)
         nc.sync.dma_start(term[0][:], terms_rows[:, 0, :])
@@ -117,13 +131,9 @@ def tile_list_slot_trade_table_kernel(
                 w4_scales[0, 4 * q : 4 * q + 4, :].bitcast(I32),
             )
 
-        def wg(t):
-            return wg_first[:] if t == 0 else wg_rest[:, t - 1, :]
-
-        v_sc0 = held([P, S], U8, "v_sc0")
-        nc.vector.tensor_copy(v_sc0[:], tab_sc[:].indirect(idx[:]))
-        nc.scalar.dma_start(v_sc1[0:112, :].bitcast(I32), v_sc0[4:116, :].bitcast(I32))
-        v_sc = [v_sc0, v_sc1]
+        v_sc = [held([P, S], U8, "v_sc%d" % a) for a in range(PASSES)]
+        for a in range(PASSES):
+            nc.vector.tensor_copy(v_sc[a][:], tab_sc[:, a, :].indirect(idx[:]))
         v_w = [[held([P, BANK], U32, "v_w%d_%d" % (a, u)) for u in range(HALVES)] for a in range(PASSES)]
 
         def gather_words(a, u):
@@ -131,93 +141,93 @@ def tile_list_slot_trade_table_kernel(
                 v_w[a][u][:], tab_w[a][:].indirect(idx[:, 32 * u : 32 * (u + 1)])
             )
 
-        w2_sc = held([P, PASSES, H], U8, "w2_sc")
+        w2_sc_cols = w2_sc_raw[:].rearrange("p a (m t) -> p a m t", t=PACK)
+        w2_sc_first = held([P, PASSES, P], U8, "w2_sc_first")
+        w2_sc_rest = held([P, PASSES, PACK - 1, P], U8, "w2_sc_rest")
         w2_w = held([P, PASSES, 2 * H], U8, "w2_w")
-        gather_words(0, 0)
-        nc.vector.tensor_copy(
-            w2_sc[:].rearrange("p a (t m) -> p a m t", t=PACK),
-            w2_sc_raw[:].rearrange("p a (m t) -> p a m t", t=PACK),
+        nc.gpsimd.tensor_copy(w2_sc_first[:], w2_sc_cols[:, :, :, 0])
+        nc.gpsimd.tensor_copy(
+            w2_sc_rest[:], w2_sc_cols[:, :, :, 1:].rearrange("p a m t -> p a t m")
         )
-        gather_words(0, 1)
-        gather_words(1, 0)
-        gather_words(1, 1)
         nc.scalar.copy(
-            w2_w[:].bitcast(U16).rearrange("p a (t m) -> p a m t", t=PACK),
-            w2_raw[:].bitcast(U16).rearrange("p a (m t) -> p a m t", t=PACK),
+            w2_w[:].bitcast(U16).rearrange("p a (t m) -> p a t m", t=PACK),
+            w2_raw[:].bitcast(U16).rearrange("p a (m t) -> p a t m", t=PACK),
         )
+        for a in range(PASSES):
+            for u in range(HALVES):
+                gather_words(a, u)
 
-        w1_bf0 = held([P, PACK, P, PACK], BF16, "w1_bf0")
-        w1_c0 = held([P, H], U32, "w1_c0")
-        w1_s0 = held([P, H], U8, "w1_s0")
-        nc.scalar.copy(
-            w1_bf0[:].rearrange("p t m j -> p m j t"),
-            w1_raw[0][:].rearrange("p j (m t) -> p m j t", t=PACK),
-        )
-        nc.vector.quantize_mx(
-            w1_c0[:].bitcast(FP8X4), w1_s0[:], w1_bf0[:].rearrange("p t m j -> p (t m j)")
-        )
-        w1_bf1a = held([P, P, PACK], BF16, "w1_bf1a")
-        w1_c1a = held([P, P], U32, "w1_c1a")
-        w1_s1a = held([P, P], U8, "w1_s1a")
-        w1_bf1b = held([P, PACK - 1, P, PACK], BF16, "w1_bf1b")
-        w1_c1b = held([P, (PACK - 1) * P], U32, "w1_c1b")
-        w1_s1b = held([P, (PACK - 1) * P], U8, "w1_s1b")
-        w1_cols = w1_raw[1][:].rearrange("p j (m t) -> p m j t", t=PACK)
-        nc.vector.tensor_copy(w1_bf1a[:], w1_cols[:, :, :, 0])
-        nc.vector.quantize_mx(
-            w1_c1a[:].bitcast(FP8X4), w1_s1a[:], w1_bf1a[:].rearrange("p m j -> p (m j)")
-        )
-
-        def w1_rest():
-            nc.scalar.copy(w1_bf1b[:].rearrange("p t m j -> p m j t"), w1_cols[:, :, :, 1:])
+        w1_cols = [w1_raw[a][:].rearrange("p j (m t) -> p m j t", t=PACK) for a in range(PASSES)]
+        w1_c_first = [held([P, P], U32, "w1_c_first%d" % a) for a in range(PASSES)]
+        w1_s_first = [held([P, P], U8, "w1_s_first%d" % a) for a in range(PASSES)]
+        work = [held([P, S], F32, "work%d" % i) for i in range(2)]
+        h_lead = held([P, BANK], F32, "h_lead")
+        w1_c_rest = [held([P, (PACK - 1) * P], U32, "w1_c_rest%d" % a) for a in range(PASSES)]
+        w1_s_both = keep.tile([P, PASSES, (PACK - 1) * P], U8, name="w1_s_both", tag="wg_first0", align_bytes=64)
+        w1_s_rest = [w1_s_both[:, a, :] for a in range(PASSES)]
+        for a in range(PASSES):
+            grouped = held([P, P, PACK], BF16, "w1_bf_first%d" % a)
+            nc.vector.tensor_copy(grouped[:], w1_cols[a][:, :, :, 0])
             nc.vector.quantize_mx(
-                w1_c1b[:].bitcast(FP8X4), w1_s1b[:], w1_bf1b[:].rearrange("p t m j -> p (t m j)")
+                w1_c_first[a][:].bitcast(FP8X4), w1_s_first[a][:],
+                grouped[:].rearrange("p m j -> p (m j)"),
             )
 
         def w1_operand(a, t):
-            if a == 0:
-                return w1_c0[:, P * t : P * (t + 1)], w1_s0[:, P * t : P * (t + 1)]
             if t == 0:
-                return w1_c1a[:], w1_s1a[:]
-            return w1_c1b[:, P * (t - 1) : P * t], w1_s1b[:, P * (t - 1) : P * t]
+                return w1_c_first[a][:], w1_s_first[a][:]
+            cols = slice(P * (t - 1), P * t)
+            return w1_c_rest[a][:, cols], w1_s_rest[a][:, cols]
 
-        def phases(t, u):
-            d2 = psum.tile([P, BANK], F32, name="scalar_bank")
-            for a in range(PASSES):
-                nc.tensor.matmul_mx(
-                    d2[:],
-                    lhsT=w2_w[:, a, 2 * P * t : 2 * P * (t + 1)].bitcast(FP4X4),
-                    lhsT_scale=w2_sc[:, a, P * t : P * (t + 1)],
-                    rhs=v_w[a][u][:].bitcast(FP8X4),
-                    rhs_scale=v_sc[a][:, BANK * u : BANK * (u + 1)],
-                    start=(a == 0),
-                    stop=(a == PASSES - 1),
-                )
-            sin_half = ring.tile([P, BANK], F32, name="sin_half")
-            nc.scalar.activation(sin_half[:], d2[:], ACT.Sin, scale=0.5)
-            sq = ring.tile([P, BANK], F32, name="sq", bufs=4)
-            nc.scalar.activation(sq[:], sin_half[:], ACT.Square)
-            return sq
+        def w2_operand(a, t):
+            codes = w2_w[:, a, 2 * P * t : 2 * P * (t + 1)]
+            return codes, (w2_sc_first[:, a, :] if t == 0 else w2_sc_rest[:, a, t - 1, :])
 
-        def features(t, u, sq, h):
-            d1 = psum.tile([P, BANK], F32, name="vector_bank")
+        def product(operand, dtype, t, u, bank):
+            acc = psum.tile([P, BANK], F32, name=bank)
             for a in range(PASSES):
-                codes, scales = w1_operand(a, t)
+                codes, scales = operand(a, t)
                 nc.tensor.matmul_mx(
-                    d1[:],
-                    lhsT=codes.bitcast(FP8X4),
+                    acc[:],
+                    lhsT=codes.bitcast(dtype),
                     lhsT_scale=scales,
                     rhs=v_w[a][u][:].bitcast(FP8X4),
                     rhs_scale=v_sc[a][:, BANK * u : BANK * (u + 1)],
                     start=(a == 0),
                     stop=(a == PASSES - 1),
                 )
-            prod = ring.tile([P, BANK], F32, name="prod")
-            nc.vector.scalar_tensor_tensor(prod[:], sq[:], -0.5, d1[:], ALU.add, ALU.mult)
-            nc.scalar.activation(
-                h[:, BANK * u : BANK * (u + 1)], prod[:], ACT.Identity,
-                bias=shift_sb[:, t : t + 1], scale=-2.0,
-            )
+            return acc
+
+        def sine_squared(t, u, sin_half):
+            d2 = product(w2_operand, FP4X4, t, u, "scalar_bank")
+            nc.scalar.activation(sin_half, d2[:], ACT.Sin, scale=0.5)
+            sq = ring.tile([P, BANK], F32, name="sq")
+            nc.scalar.activation(sq[:], sin_half, ACT.Square)
+            return sq
+
+        def factors(t):
+            pairs = []
+            for u in range(HALVES):
+                sin_half = ring.tile([P, BANK], F32, name="sin_half")
+                sq = sine_squared(t, u, sin_half[:])
+                cosine = ring.tile([P, BANK], F32, name="cosine", bufs=4)
+                nc.scalar.activation(cosine[:], sq[:], ACT.Identity, bias=1.0, scale=-2.0)
+                d1 = product(w1_operand, FP8X4, t, u, "vector_bank")
+                amp = ring.tile([P, BANK], F32, name="amp", bufs=4)
+                nc.scalar.copy(amp[:], d1[:])
+                pairs.append((cosine, amp))
+            return pairs
+
+        def features(t, pairs, prod, h):
+            bias = shift_sb[:, t : t + 1]
+            halves = [slice(BANK * u, BANK * (u + 1)) for u in range(HALVES)]
+            for cols, (cosine, amp) in zip(halves, pairs):
+                nc.gpsimd.tensor_tensor(prod[:, cols], cosine[:], amp[:], ALU.mult)
+            for cols in halves:
+                if t == ORDER[1]:
+                    nc.scalar.activation(h[:, cols], prod[:, cols], ACT.Identity, bias=bias)
+                else:
+                    nc.gpsimd.tensor_scalar(h[:, cols], prod[:, cols], 1.0, bias, ALU.mult, ALU.add)
 
         page_bf = [held([P, BANK, PACK], BF16, "page_bf%d" % c) for c in range(CHUNKS)]
 
@@ -225,48 +235,78 @@ def tile_list_slot_trade_table_kernel(
             engine_copy(page_bf[c][:, :, t], page[t][:, BANK * c : BANK * (c + 1)])
 
         t0 = ORDER[0]
-        h = ring.tile([P, S], F32, name="h")
-        sqs = [phases(t0, u) for u in range(HALVES)]
+        rest_words = (PACK - 1) * P * PACK // 2
+        scratch = held([P, PASSES * rest_words], F32, "scratch")
+        sqs = [sine_squared(t0, u, scratch[:, BANK * u : BANK * (u + 1)]) for u in range(HALVES)]
+        h_first = [h_lead[:], work[0][:, BANK // 2 : BANK // 2 + BANK]]
         for u in range(HALVES):
-            features(t0, u, sqs[u], h)
-        w1_rest()
+            d1 = product(w1_operand, FP8X4, t0, u, "vector_bank")
+            nc.vector.scalar_tensor_tensor(h_first[u], sqs[u][:], -0.5, d1[:], ALU.add, ALU.mult)
+        for u in range(HALVES):
+            nc.vector.tensor_scalar(
+                h_first[u], h_first[u], -2.0, shift_sb[:, t0 : t0 + 1], ALU.mult, ALU.add
+            )
+
+        def put_half(u):
+            nc.vector.tensor_tensor(
+                page[t0][:].indirect(idx2[:, 32 * u : 32 * (u + 1)]),
+                h_first[u], wg_first[u][:], ALU.mult,
+            )
+
+        put_half(0)
+        for a in range(PASSES):
+            grouped = scratch[:, rest_words * a : rest_words * (a + 1)].bitcast(BF16)
+            nc.scalar.copy(
+                grouped.rearrange("p (t m j) -> p m j t", m=P, j=PACK), w1_cols[a][:, :, :, 1:]
+            )
+            nc.vector.quantize_mx(w1_c_rest[a][:].bitcast(FP8X4), w1_s_rest[a], grouped)
+        put_half(1)
 
         w3_bf = held([P, N, PACK], BF16, "w3_bf")
         w3_c = held([P, N], U32, "w3_c")
         w3_s = held([P, N], U8, "w3_s")
 
+        def put_low(t, low):
+            nc.vector.tensor_copy(page[t][:].indirect(idx4[:]), low[:])
+
+        pending = None
+        pairs = factors(ORDER[1])
         for step, t in enumerate(ORDER):
             nxt = ORDER[step + 1] if step + 1 < PACK else None
-            nc.vector.tensor_tensor(page[t][:].indirect(idx2[:]), h[:], wg(t), ALU.mult)
+            evening = ring.tile([P, NPAIR], F32, name="evening")
+            morning = ring.tile([P, NPAIR], F32, name="morning")
+            prod, h = work[step % 2], work[(step + 1) % 2]
+            traded = prod[:, BANK // 2 : BANK // 2 + NPAIR]
+            low = ring.tile([P, NPAIR], F32, name="low")
+            high = ring.tile([P, NPAIR], F32, name="high")
             if nxt is not None:
-                h = ring.tile([P, S], F32, name="h")
-                sqs = [phases(nxt, u) for u in range(HALVES)]
-                features(nxt, 0, sqs[0], h)
+                features(nxt, pairs, prod, h)
+            nc.vector.tensor_copy(evening[:], page[t][:].indirect(idx4[:]))
+            nc.vector.tensor_copy(morning[:], page[t][:].indirect(idx3[:]))
+            adder = nc.vector if step == 0 else nc.gpsimd
+            adder.tensor_tensor(traded, evening[:], term[t][:], ALU.add)
+            if step + 2 < PACK:
+                pairs = factors(ORDER[step + 2])
+            if pending is not None:
+                put_low(*pending)
+                for c in range(CHUNKS):
+                    round_page(pending[0], c, nc.scalar.copy)
+            nc.vector.tensor_tensor(low[:], morning[:], evening[:], ALU.min)
+            nc.vector.tensor_tensor(high[:], morning[:], traded, ALU.max)
+            if nxt is not None:
+                nc.vector.tensor_tensor(page[nxt][:].indirect(idx2[:]), h[:], wg_rest[:, nxt - 1, :], ALU.mult)
             else:
+                nc.vector.quantize_mx(
+                    w3_c[:].bitcast(FP8X4), w3_s[:], w3_bf[:].rearrange("p c j -> p (c j)")
+                )
+            nc.vector.tensor_copy(page[t][:].indirect(idx3[:]), high[:])
+            if step == 1:
                 nc.scalar.copy(
                     w3_bf[:].rearrange("p (c i) j -> p c j i", i=4),
                     w3_raw[:].rearrange("p j (c i) -> p c j i", i=4),
                 )
-                nc.vector.quantize_mx(
-                    w3_c[:].bitcast(FP8X4), w3_s[:], w3_bf[:].rearrange("p c j -> p (c j)")
-                )
-            evening = ring.tile([P, NPAIR], F32, name="evening")
-            morning = ring.tile([P, NPAIR], F32, name="morning")
-            traded = ring.tile([P, NPAIR], F32, name="traded")
-            low = ring.tile([P, NPAIR], F32, name="low")
-            high = ring.tile([P, NPAIR], F32, name="high")
-            nc.vector.tensor_copy(evening[:], page[t][:].indirect(idx4[:]))
-            nc.vector.tensor_copy(morning[:], page[t][:].indirect(idx3[:]))
-            nc.vector.tensor_tensor(traded[:], evening[:], term[t][:], ALU.add)
-            nc.vector.tensor_tensor(low[:], morning[:], evening[:], ALU.min)
-            nc.vector.tensor_tensor(high[:], morning[:], traded[:], ALU.max)
-            nc.vector.tensor_copy(page[t][:].indirect(idx4[:]), low[:])
-            if nxt is not None:
-                features(nxt, 1, sqs[1], h)
-            nc.vector.tensor_copy(page[t][:].indirect(idx3[:]), high[:])
-            if nxt is not None:
-                for c in range(CHUNKS):
-                    round_page(t, c, nc.scalar.copy)
+            pending = (t, low)
+        put_low(*pending)
 
         last = ORDER[-1]
         for c in range(CHUNKS):

@@ -18,14 +18,20 @@ ACT = mybir.ActivationFunctionType
 
 P = 128
 PACK = 4
-PASSES = K // (P * PACK)
+K_PASS = P * PACK
+PASSES = K // K_PASS
 BANK = 512
 HALVES = S // BANK
+LIST_COLS = BANK // 16
 CHUNKS = T2 // BANK
-NT = N // P
+N_TILES = N // P
 QUADS = 4
+QUAD = P // QUADS
+SCALE_ROWS = 4
+REST = PACK - 1
 ORDER = (0, 2, 3, 1)
 VECTOR_CHUNKS = 2
+SHIFT_ROWS = 112
 
 
 def tile_list_slot_trade_table_kernel(
@@ -33,41 +39,39 @@ def tile_list_slot_trade_table_kernel(
     shift, wgs, page0, terms, w3, w4_words, w4_scales, out,
 ):
     nc = tc.nc
+    first, last = ORDER[0], ORDER[-1]
     with ExitStack() as ctx:
         keep = ctx.enter_context(tc.tile_pool(name="keep", bufs=1))
         ring = ctx.enter_context(tc.tile_pool(name="ring", bufs=2))
-        psum = ctx.enter_context(tc.psum_pool(name="psum", bufs=4))
+        psum = ctx.enter_context(tc.psum_pool(name="psum", bufs=1))
 
-        def held(shape, dtype, name):
-            return keep.tile(shape, dtype, name=name, align_bytes=64)
+        def held(shape, dtype, name, tag=None):
+            return keep.tile(shape, dtype, name=name, tag=tag or name, align_bytes=64)
+
+        def bank_cols(i):
+            return slice(BANK * i, BANK * (i + 1))
+
+        def load_scale_rows(tile, scales):
+            for q in range(QUADS):
+                rows = scales[:, SCALE_ROWS * q : SCALE_ROWS * (q + 1), :]
+                nc.sync.dma_start(
+                    tile[QUAD * q : QUAD * q + SCALE_ROWS, :, :].bitcast(I32),
+                    rows.rearrange("a r c -> r a c").bitcast(I32),
+                )
 
         idx = held([P, S // 16], U16, "idx")
         idx2 = held([P, S // 16], U16, "idx2")
         idx3 = held([P, NPAIR // 16], U16, "idx3")
         idx4 = held([P, NPAIR // 16], U16, "idx4")
 
-        tab_sc = held([P, PASSES, T], U8, "tab_sc")
+        tab_sc = held([P, T], U8, "tab_sc")
+        v_sc = [held([P, S], U8, "v_sc%d" % a) for a in range(PASSES)]
         w2_sc_raw = held([P, PASSES, H], U8, "w2_sc_raw")
-        w4_sc = held([P, N], U8, "w4_sc")
-        nc.gpsimd.memset(tab_sc[:, 0, :].bitcast(I32), 0)
-        nc.vector.memset(tab_sc[:, 1, :].bitcast(I32), 0)
+        w4_sc = held([P, 1, N], U8, "w4_sc")
+        nc.gpsimd.memset(tab_sc[:].bitcast(I32), 0)
         nc.gpsimd.memset(w2_sc_raw[:].rearrange("p a c -> p (a c)").bitcast(I32), 0)
-        nc.vector.memset(w4_sc[:].bitcast(I32), 0)
-
-        tab_w = [held([P, T], U32, "tab_w%d" % a) for a in range(PASSES)]
-        w1_raw = [held([P, PACK, H], F32, "w1_raw%d" % a) for a in range(PASSES)]
-
-        def load_words(a):
-            nc.sync.dma_start(
-                tab_w[a][:].bitcast(I32),
-                tab_words[a].rearrange("p t i -> p (t i)").bitcast(I32),
-            )
-
-        def load_w1(a):
-            nc.sync.dma_start(
-                w1_raw[a][:],
-                w1[512 * a : 512 * (a + 1), :].rearrange("(p j) c -> p j c", j=PACK),
-            )
+        nc.vector.memset(v_sc[1][:].bitcast(I32), 0)
+        nc.vector.memset(w4_sc[:, 0, :].bitcast(I32), 0)
 
         w2_raw = held([P, PASSES, 2 * H], U8, "w2_raw")
         nc.sync.dma_start(
@@ -75,47 +79,47 @@ def tile_list_slot_trade_table_kernel(
         )
         for q in range(QUADS):
             nc.sync.dma_start(
-                tab_sc[32 * q : 32 * q + 4, :, :].bitcast(I32),
-                tab_scales[:, 4 * q : 4 * q + 4, :].rearrange("a r t -> r a t").bitcast(I32),
+                tab_sc[QUAD * q : QUAD * q + PASSES * SCALE_ROWS, :].bitcast(I32),
+                tab_scales[:, SCALE_ROWS * q : SCALE_ROWS * (q + 1), :].bitcast(I32),
             )
         nc.sync.dma_start(idx[:], offs)
-        load_words(0)
-        load_words(1)
-        for q in range(QUADS):
+        tab_w = [held([P, T], U32, "tab_w%d" % a) for a in range(PASSES)]
+        for a in range(PASSES):
             nc.sync.dma_start(
-                w2_sc_raw[32 * q : 32 * q + 4, :, :].bitcast(I32),
-                w2_scales[:, 4 * q : 4 * q + 4, :].rearrange("a r c -> r a c").bitcast(I32),
+                tab_w[a][:].bitcast(I32),
+                tab_words[a].rearrange("p t i -> p (t i)").bitcast(I32),
             )
-        load_w1(0)
-        load_w1(1)
+        load_scale_rows(w2_sc_raw, w2_scales)
+        w1_raw = [held([P, PACK, H], F32, "w1_raw%d" % a) for a in range(PASSES)]
+        for a in range(PASSES):
+            nc.sync.dma_start(
+                w1_raw[a][:],
+                w1[K_PASS * a : K_PASS * (a + 1), :].rearrange("(p j) c -> p j c", j=PACK),
+            )
         shift_sb = held([P, PACK], F32, "shift_sb")
         nc.sync.dma_start(shift_sb[:], shift.rearrange("(p t) -> p t", t=PACK))
+        nc.sync.dma_start(idx2[:], offs2)
 
         wgs_rows = wgs.rearrange("(q t) j -> q t j", t=PACK)
-        wg_first = [
-            keep.tile([P, BANK], F32, name="wg_first%d" % u, tag="wg_first%d" % u, align_bytes=64)
-            for u in range(HALVES)
-        ]
+        wg_first = [held([P, BANK], F32, "wg_first%d" % u) for u in range(HALVES)]
+        wg_rest = held([P, REST, S], F32, "wg_rest")
 
-        def load_wg_first(u):
-            cols = slice(BANK * u, BANK * (u + 1))
+        def load_wgs(tile, rows):
             for q in range(QUADS):
-                nc.sync.dma_start(wg_first[u][32 * q : 32 * q + 32, :], wgs_rows[:, 0, cols])
+                nc.sync.dma_start(tile[QUAD * q : QUAD * (q + 1)], rows)
 
-        nc.sync.dma_start(idx2[:], offs2)
-        load_wg_first(0)
-        page_rows = page0.rearrange("(p t) c -> p t c", t=PACK)
-        terms_rows = terms.rearrange("(p t) m -> p t m", t=PACK)
         page = [held([P, T2], F32, "page%d" % t) for t in range(PACK)]
         term = [held([P, NPAIR], F32, "term%d" % t) for t in range(PACK)]
-        nc.sync.dma_start(page[0][:], page_rows[:, 0, :])
-        load_wg_first(1)
+        page_rows = page0.rearrange("(p t) c -> p t c", t=PACK)
+        terms_rows = terms.rearrange("(p t) m -> p t m", t=PACK)
+
+        load_wgs(wg_first[0], wgs_rows[:, first, bank_cols(0)])
+        nc.sync.dma_start(page[first][:], page_rows[:, first, :])
+        load_wgs(wg_first[1], wgs_rows[:, first, bank_cols(1)])
         nc.sync.dma_start(idx4[:], offs4)
         nc.sync.dma_start(idx3[:], offs3)
-        nc.sync.dma_start(term[0][:], terms_rows[:, 0, :])
-        wg_rest = held([P, PACK - 1, S], F32, "wg_rest")
-        for q in range(QUADS):
-            nc.sync.dma_start(wg_rest[32 * q : 32 * q + 32, :, :], wgs_rows[:, 1:, :])
+        nc.sync.dma_start(term[first][:], terms_rows[:, first, :])
+        load_wgs(wg_rest, wgs_rows[:, 1:, :])
         for t in ORDER[1:]:
             nc.sync.dma_start(page[t][:], page_rows[:, t, :])
             nc.sync.dma_start(term[t][:], terms_rows[:, t, :])
@@ -125,160 +129,169 @@ def tile_list_slot_trade_table_kernel(
         nc.sync.dma_start(
             w4_w[:].bitcast(I32), w4_words[0].rearrange("p c i -> p (c i)").bitcast(I32)
         )
-        for q in range(QUADS):
-            nc.sync.dma_start(
-                w4_sc[32 * q : 32 * q + 4, :].bitcast(I32),
-                w4_scales[0, 4 * q : 4 * q + 4, :].bitcast(I32),
-            )
+        load_scale_rows(w4_sc, w4_scales)
 
-        v_sc = [held([P, S], U8, "v_sc%d" % a) for a in range(PASSES)]
-        for a in range(PASSES):
-            nc.vector.tensor_copy(v_sc[a][:], tab_sc[:, a, :].indirect(idx[:]))
-        v_w = [[held([P, BANK], U32, "v_w%d_%d" % (a, u)) for u in range(HALVES)] for a in range(PASSES)]
+        nc.vector.tensor_copy(v_sc[0][:], tab_sc[:].indirect(idx[:]))
+        nc.scalar.dma_start(
+            v_sc[1][0:SHIFT_ROWS, :].bitcast(I32),
+            v_sc[0][SCALE_ROWS : SCALE_ROWS + SHIFT_ROWS, :].bitcast(I32),
+        )
+        v_sc_for_w2 = [v_sc[a][:] for a in range(PASSES)]
+        v_sc_for_w1 = [v_sc[0][SCALE_ROWS * a :, :] for a in range(PASSES)]
 
-        def gather_words(a, u):
-            nc.vector.tensor_copy(
-                v_w[a][u][:], tab_w[a][:].indirect(idx[:, 32 * u : 32 * (u + 1)])
-            )
-
-        w2_sc_cols = w2_sc_raw[:].rearrange("p a (m t) -> p a m t", t=PACK)
-        w2_sc_first = held([P, PASSES, P], U8, "w2_sc_first")
-        w2_sc_rest = held([P, PASSES, PACK - 1, P], U8, "w2_sc_rest")
         w2_w = held([P, PASSES, 2 * H], U8, "w2_w")
-        nc.gpsimd.tensor_copy(w2_sc_first[:], w2_sc_cols[:, :, :, 0])
-        nc.gpsimd.tensor_copy(
-            w2_sc_rest[:], w2_sc_cols[:, :, :, 1:].rearrange("p a m t -> p a t m")
-        )
-        nc.scalar.copy(
-            w2_w[:].bitcast(U16).rearrange("p a (t m) -> p a t m", t=PACK),
-            w2_raw[:].bitcast(U16).rearrange("p a (m t) -> p a t m", t=PACK),
-        )
+        w2_sc_cols = w2_sc_raw[:].rearrange("p a (m t) -> p a t m", t=PACK)
+        w2_sc_first = held([P, PASSES, P], U8, "w2_sc_first")
+        w2_sc_rest = held([P, PASSES, REST, P], U8, "w2_sc_rest")
+        for a in range(PASSES):
+            nc.gpsimd.tensor_copy(
+                w2_w[:, a, :].rearrange("p (t m b) -> p t m b", t=PACK, b=2),
+                w2_raw[:, a, :].rearrange("p (m t b) -> p t m b", t=PACK, b=2),
+            )
+        nc.gpsimd.tensor_copy(w2_sc_first[:], w2_sc_cols[:, :, first, :])
+        nc.gpsimd.tensor_copy(w2_sc_rest[:], w2_sc_cols[:, :, 1:, :])
+
+        v_w = [
+            [held([P, BANK], U32, "v_w%d_%d" % (a, u)) for u in range(HALVES)]
+            for a in range(PASSES)
+        ]
         for a in range(PASSES):
             for u in range(HALVES):
-                gather_words(a, u)
+                nc.vector.tensor_copy(
+                    v_w[a][u][:], tab_w[a][:].indirect(idx[:, LIST_COLS * u : LIST_COLS * (u + 1)])
+                )
 
         w1_cols = [w1_raw[a][:].rearrange("p j (m t) -> p m j t", t=PACK) for a in range(PASSES)]
         w1_c_first = [held([P, P], U32, "w1_c_first%d" % a) for a in range(PASSES)]
         w1_s_first = [held([P, P], U8, "w1_s_first%d" % a) for a in range(PASSES)]
-        work = [held([P, S], F32, "work%d" % i) for i in range(2)]
-        h_lead = held([P, BANK], F32, "h_lead")
-        w1_c_rest = [held([P, (PACK - 1) * P], U32, "w1_c_rest%d" % a) for a in range(PASSES)]
-        w1_s_both = keep.tile([P, PASSES, (PACK - 1) * P], U8, name="w1_s_both", tag="wg_first0", align_bytes=64)
-        w1_s_rest = [w1_s_both[:, a, :] for a in range(PASSES)]
+        w1_c_rest = [held([P, REST * P], U32, "w1_c_rest%d" % a) for a in range(PASSES)]
+        w1_s_rest = held([P, PASSES, REST * P], U8, "w1_s_rest", tag="wg_first0")
         for a in range(PASSES):
-            grouped = held([P, P, PACK], BF16, "w1_bf_first%d" % a)
-            nc.vector.tensor_copy(grouped[:], w1_cols[a][:, :, :, 0])
+            w1_bf_first = held([P, P, PACK], BF16, "w1_bf_first%d" % a)
+            nc.vector.tensor_copy(w1_bf_first[:], w1_cols[a][:, :, :, first])
             nc.vector.quantize_mx(
                 w1_c_first[a][:].bitcast(FP8X4), w1_s_first[a][:],
-                grouped[:].rearrange("p m j -> p (m j)"),
+                w1_bf_first[:].rearrange("p m j -> p (m j)"),
             )
 
         def w1_operand(a, t):
-            if t == 0:
+            if t == first:
                 return w1_c_first[a][:], w1_s_first[a][:]
             cols = slice(P * (t - 1), P * t)
-            return w1_c_rest[a][:, cols], w1_s_rest[a][:, cols]
+            return w1_c_rest[a][:, cols], w1_s_rest[:, a, cols]
 
         def w2_operand(a, t):
             codes = w2_w[:, a, 2 * P * t : 2 * P * (t + 1)]
-            return codes, (w2_sc_first[:, a, :] if t == 0 else w2_sc_rest[:, a, t - 1, :])
+            return codes, (w2_sc_first[:, a, :] if t == first else w2_sc_rest[:, a, t - 1, :])
 
-        def product(operand, dtype, t, u, bank):
-            acc = psum.tile([P, BANK], F32, name=bank)
+        banks = [psum.tile([P, BANK], F32, name="bank%d" % b) for b in range(8)]
+
+        def product(operand, dtype, v_scales, step, u, pair):
+            acc = banks[HALVES * (pair % 2) + u]
             for a in range(PASSES):
-                codes, scales = operand(a, t)
+                codes, scales = operand(a, ORDER[step])
                 nc.tensor.matmul_mx(
                     acc[:],
                     lhsT=codes.bitcast(dtype),
                     lhsT_scale=scales,
                     rhs=v_w[a][u][:].bitcast(FP8X4),
-                    rhs_scale=v_sc[a][:, BANK * u : BANK * (u + 1)],
+                    rhs_scale=v_scales[a][:, bank_cols(u)],
                     start=(a == 0),
                     stop=(a == PASSES - 1),
                 )
             return acc
 
-        def sine_squared(t, u, sin_half):
-            d2 = product(w2_operand, FP4X4, t, u, "scalar_bank")
-            nc.scalar.activation(sin_half, d2[:], ACT.Sin, scale=0.5)
+        def sine_squared(step, u, sin_half):
+            phase = product(w2_operand, FP4X4, v_sc_for_w2, step, u, step)
+            nc.scalar.activation(sin_half, phase[:], ACT.Sin, scale=0.5)
             sq = ring.tile([P, BANK], F32, name="sq")
             nc.scalar.activation(sq[:], sin_half, ACT.Square)
             return sq
 
-        def factors(t):
+        def amplitude(step, u):
+            return product(w1_operand, FP8X4, v_sc_for_w1, step, u, step + 1)
+
+        def factors(step):
             pairs = []
             for u in range(HALVES):
                 sin_half = ring.tile([P, BANK], F32, name="sin_half")
-                sq = sine_squared(t, u, sin_half[:])
-                cosine = ring.tile([P, BANK], F32, name="cosine", bufs=4)
+                sq = sine_squared(step, u, sin_half[:])
+                cosine = ring.tile([P, BANK], F32, name="cosine", bufs=2 * HALVES)
                 nc.scalar.activation(cosine[:], sq[:], ACT.Identity, bias=1.0, scale=-2.0)
-                d1 = product(w1_operand, FP8X4, t, u, "vector_bank")
-                amp = ring.tile([P, BANK], F32, name="amp", bufs=4)
-                nc.scalar.copy(amp[:], d1[:])
+                amp = ring.tile([P, BANK], F32, name="amp", bufs=2 * HALVES)
+                nc.scalar.copy(amp[:], amplitude(step, u)[:])
                 pairs.append((cosine, amp))
             return pairs
 
+        rest_words = REST * P * PACK // 2
+        scratch = [
+            held([P, rest_words], F32, "scratch")[:],
+            w1_raw[0][:].rearrange("p j c -> p (j c)")[:, 0:rest_words],
+        ]
+        sqs = []
+        for u in range(HALVES):
+            sqs.append(sine_squared(0, u, scratch[u][:, 0:BANK]))
+            nc.scalar.copy(
+                scratch[u].bitcast(BF16).rearrange("p (t m j) -> p m j t", m=P, j=PACK),
+                w1_cols[u][:, :, :, 1:],
+            )
+        work = [held([P, S], F32, "work%d" % i) for i in range(2)]
+        middle = slice(BANK // 2, BANK // 2 + BANK)
+        h_first = [held([P, BANK], F32, "h_lead")[:], work[0][:, middle]]
+        for u in range(HALVES):
+            nc.vector.scalar_tensor_tensor(
+                h_first[u], sqs[u][:], -0.5, amplitude(0, u)[:], ALU.add, ALU.mult
+            )
+        for u in range(HALVES):
+            nc.vector.tensor_scalar(
+                h_first[u], h_first[u], -2.0, shift_sb[:, first : first + 1], ALU.mult, ALU.add
+            )
+
+        def put_first_half(u):
+            nc.vector.tensor_tensor(
+                page[first][:].indirect(idx2[:, LIST_COLS * u : LIST_COLS * (u + 1)]),
+                h_first[u], wg_first[u][:], ALU.mult,
+            )
+
+        put_first_half(0)
+        for a in range(PASSES):
+            nc.vector.quantize_mx(
+                w1_c_rest[a][:].bitcast(FP8X4), w1_s_rest[:, a, :], scratch[a].bitcast(BF16)
+            )
+        put_first_half(1)
+
+        page_bf = [held([P, BANK, PACK], BF16, "page_bf%d" % c) for c in range(CHUNKS)]
+        w3_bf = held([P, N, PACK], BF16, "w3_bf")
+        w3_c = held([P, N], U32, "w3_c")
+        w3_s = held([P, N], U8, "w3_s")
+
+        def round_page(t, c, copy):
+            copy(page_bf[c][:, :, t], page[t][:, bank_cols(c)])
+
         def features(t, pairs, prod, h):
             bias = shift_sb[:, t : t + 1]
-            halves = [slice(BANK * u, BANK * (u + 1)) for u in range(HALVES)]
-            for cols, (cosine, amp) in zip(halves, pairs):
-                nc.gpsimd.tensor_tensor(prod[:, cols], cosine[:], amp[:], ALU.mult)
-            for cols in halves:
+            for u, (cosine, amp) in enumerate(pairs):
+                nc.gpsimd.tensor_tensor(prod[:, bank_cols(u)], cosine[:], amp[:], ALU.mult)
+            for u in range(HALVES):
+                cols = bank_cols(u)
                 if t == ORDER[1]:
                     nc.scalar.activation(h[:, cols], prod[:, cols], ACT.Identity, bias=bias)
                 else:
                     nc.gpsimd.tensor_scalar(h[:, cols], prod[:, cols], 1.0, bias, ALU.mult, ALU.add)
 
-        page_bf = [held([P, BANK, PACK], BF16, "page_bf%d" % c) for c in range(CHUNKS)]
-
-        def round_page(t, c, engine_copy):
-            engine_copy(page_bf[c][:, :, t], page[t][:, BANK * c : BANK * (c + 1)])
-
-        t0 = ORDER[0]
-        rest_words = (PACK - 1) * P * PACK // 2
-        scratch = held([P, PASSES * rest_words], F32, "scratch")
-        sqs = [sine_squared(t0, u, scratch[:, BANK * u : BANK * (u + 1)]) for u in range(HALVES)]
-        h_first = [h_lead[:], work[0][:, BANK // 2 : BANK // 2 + BANK]]
-        for u in range(HALVES):
-            d1 = product(w1_operand, FP8X4, t0, u, "vector_bank")
-            nc.vector.scalar_tensor_tensor(h_first[u], sqs[u][:], -0.5, d1[:], ALU.add, ALU.mult)
-        for u in range(HALVES):
-            nc.vector.tensor_scalar(
-                h_first[u], h_first[u], -2.0, shift_sb[:, t0 : t0 + 1], ALU.mult, ALU.add
-            )
-
-        def put_half(u):
-            nc.vector.tensor_tensor(
-                page[t0][:].indirect(idx2[:, 32 * u : 32 * (u + 1)]),
-                h_first[u], wg_first[u][:], ALU.mult,
-            )
-
-        put_half(0)
-        for a in range(PASSES):
-            grouped = scratch[:, rest_words * a : rest_words * (a + 1)].bitcast(BF16)
-            nc.scalar.copy(
-                grouped.rearrange("p (t m j) -> p m j t", m=P, j=PACK), w1_cols[a][:, :, :, 1:]
-            )
-            nc.vector.quantize_mx(w1_c_rest[a][:].bitcast(FP8X4), w1_s_rest[a], grouped)
-        put_half(1)
-
-        w3_bf = held([P, N, PACK], BF16, "w3_bf")
-        w3_c = held([P, N], U32, "w3_c")
-        w3_s = held([P, N], U8, "w3_s")
-
         def put_low(t, low):
             nc.vector.tensor_copy(page[t][:].indirect(idx4[:]), low[:])
 
         pending = None
-        pairs = factors(ORDER[1])
+        pairs = factors(1)
         for step, t in enumerate(ORDER):
-            nxt = ORDER[step + 1] if step + 1 < PACK else None
+            nxt = ORDER[step + 1] if step < REST else None
             evening = ring.tile([P, NPAIR], F32, name="evening")
             morning = ring.tile([P, NPAIR], F32, name="morning")
-            prod, h = work[step % 2], work[(step + 1) % 2]
-            traded = prod[:, BANK // 2 : BANK // 2 + NPAIR]
             low = ring.tile([P, NPAIR], F32, name="low")
             high = ring.tile([P, NPAIR], F32, name="high")
+            prod, h = work[step % 2], work[(step + 1) % 2]
+            traded = prod[:, middle]
             if nxt is not None:
                 features(nxt, pairs, prod, h)
             nc.vector.tensor_copy(evening[:], page[t][:].indirect(idx4[:]))
@@ -286,7 +299,7 @@ def tile_list_slot_trade_table_kernel(
             adder = nc.vector if step == 0 else nc.gpsimd
             adder.tensor_tensor(traded, evening[:], term[t][:], ALU.add)
             if step + 2 < PACK:
-                pairs = factors(ORDER[step + 2])
+                pairs = factors(step + 2)
             if pending is not None:
                 put_low(*pending)
                 for c in range(CHUNKS):
@@ -294,7 +307,9 @@ def tile_list_slot_trade_table_kernel(
             nc.vector.tensor_tensor(low[:], morning[:], evening[:], ALU.min)
             nc.vector.tensor_tensor(high[:], morning[:], traded, ALU.max)
             if nxt is not None:
-                nc.vector.tensor_tensor(page[nxt][:].indirect(idx2[:]), h[:], wg_rest[:, nxt - 1, :], ALU.mult)
+                nc.vector.tensor_tensor(
+                    page[nxt][:].indirect(idx2[:]), h[:], wg_rest[:, nxt - 1, :], ALU.mult
+                )
             else:
                 nc.vector.quantize_mx(
                     w3_c[:].bitcast(FP8X4), w3_s[:], w3_bf[:].rearrange("p c j -> p (c j)")
@@ -308,7 +323,6 @@ def tile_list_slot_trade_table_kernel(
             pending = (t, low)
         put_low(*pending)
 
-        last = ORDER[-1]
         for c in range(CHUNKS):
             round_page(last, c, nc.vector.tensor_copy if c < VECTOR_CHUNKS else nc.scalar.copy)
         page_c = [held([P, BANK], U32, "page_c%d" % c) for c in range(CHUNKS)]
@@ -319,22 +333,22 @@ def tile_list_slot_trade_table_kernel(
                 page_bf[c][:].rearrange("p c j -> p (c j)"),
             )
         for c in range(CHUNKS):
-            for n in range(NT):
-                cols = slice(P * n, P * (n + 1))
-                e1 = psum.tile([P, BANK], F32, name="scalar_bank")
-                e2 = psum.tile([P, BANK], F32, name="vector_bank")
-                for acc, codes, scales in ((e1, w3_c, w3_s), (e2, w4_w, w4_sc)):
+            for n in range(N_TILES):
+                rows = slice(P * n, P * (n + 1))
+                turn = (N_TILES * c + n) % 4
+                e1, e2 = banks[turn], banks[4 + turn]
+                for acc, codes, scales in ((e1, w3_c, w3_s[:]), (e2, w4_w, w4_sc[:, 0, :])):
                     nc.tensor.matmul_mx(
                         acc[:],
-                        lhsT=codes[:, cols].bitcast(FP8X4),
-                        lhsT_scale=scales[:, cols],
+                        lhsT=codes[:, rows].bitcast(FP8X4),
+                        lhsT_scale=scales[:, rows],
                         rhs=page_c[c][:].bitcast(FP8X4),
                         rhs_scale=page_s[c][:],
                         start=True,
                         stop=True,
                     )
-                first = ring.tile([P, BANK], F32, name="first", bufs=3)
-                nc.scalar.copy(first[:], e1[:])
+                e1_sb = ring.tile([P, BANK], F32, name="e1_sb", bufs=3)
+                nc.scalar.copy(e1_sb[:], e1[:])
                 best = ring.tile([P, BANK], F32, name="best", bufs=6)
-                nc.vector.tensor_tensor(best[:], e2[:], first[:], ALU.max)
-                nc.sync.dma_start(out[cols, BANK * c : BANK * (c + 1)], best[:])
+                nc.vector.tensor_tensor(best[:], e2[:], e1_sb[:], ALU.max)
+                nc.sync.dma_start(out[rows, bank_cols(c)], best[:])

@@ -201,12 +201,10 @@ def tile_list_slot_trade_table_kernel(
                 )
             return acc
 
-        def sine_squared(step, u, sin_half):
+        def sine_squared(step, u, sin_half, sq):
             phase = product(w2_operand, FP4X4, v_sc_for_w2, step, u, step)
             nc.scalar.activation(sin_half, phase[:], ACT.Sin, scale=0.5)
-            sq = ring.tile([P, BANK], F32, name="sq")
-            nc.scalar.activation(sq[:], sin_half, ACT.Square)
-            return sq
+            nc.scalar.activation(sq, sin_half, ACT.Square)
 
         def amplitude(step, u):
             return product(w1_operand, FP8X4, v_sc_for_w1, step, u, step + 1)
@@ -214,40 +212,45 @@ def tile_list_slot_trade_table_kernel(
         def factors(step):
             pairs = []
             for u in range(HALVES):
-                sin_half = ring.tile([P, BANK], F32, name="sin_half")
-                sq = sine_squared(step, u, sin_half[:])
+                if (step, u) == (1, 0):
+                    sin_half, sq = w1_raw[1][:, 0, :], w1_raw[0][:, 0, :]
+                else:
+                    sin_half = ring.tile([P, BANK], F32, name="sin_half")[:]
+                    sq = ring.tile([P, BANK], F32, name="sq")[:]
+                sine_squared(step, u, sin_half, sq)
                 cosine = ring.tile([P, BANK], F32, name="cosine", bufs=2 * HALVES)
-                nc.scalar.activation(cosine[:], sq[:], ACT.Identity, bias=1.0, scale=-2.0)
+                nc.scalar.activation(cosine[:], sq, ACT.Identity, bias=1.0, scale=-2.0)
                 amp = ring.tile([P, BANK], F32, name="amp", bufs=2 * HALVES)
                 nc.scalar.copy(amp[:], amplitude(step, u)[:])
                 pairs.append((cosine, amp))
             return pairs
 
         rest_words = REST * P * PACK // 2
-        scratch = [
-            held([P, rest_words], F32, "scratch")[:],
-            w1_raw[0][:].rearrange("p j c -> p (j c)")[:, 0:rest_words],
+        stage = held([P, PASSES * rest_words], F32, "stage")
+        w1_bf_rest = [
+            stage[:, rest_words * a : rest_words * (a + 1)].bitcast(BF16) for a in range(PASSES)
         ]
-        sqs = []
-        for u in range(HALVES):
-            sqs.append(sine_squared(0, u, scratch[u][:, 0:BANK]))
-            nc.scalar.copy(
-                scratch[u].bitcast(BF16).rearrange("p (t m j) -> p m j t", m=P, j=PACK),
-                w1_cols[u][:, :, :, 1:],
-            )
-        work = [held([P, S], F32, "work%d" % i) for i in range(2)]
         middle = slice(BANK // 2, BANK // 2 + BANK)
+        work = [stage[:, BANK // 2 : BANK // 2 + S], held([P, S], F32, "work1")[:]]
         h_first = [held([P, BANK], F32, "h_lead")[:], work[0][:, middle]]
+        sq_first = [ring.tile([P, BANK], F32, name="sq")[:] for u in range(HALVES)]
+        for u in range(HALVES):
+            sine_squared(0, u, stage[:, bank_cols(u)], sq_first[u])
+        for a in range(PASSES):
+            nc.scalar.copy(
+                w1_bf_rest[a].rearrange("p (t m j) -> p m j t", m=P, j=PACK),
+                w1_cols[a][:, :, :, 1:],
+            )
         for u in range(HALVES):
             nc.vector.scalar_tensor_tensor(
-                h_first[u], sqs[u][:], -0.5, amplitude(0, u)[:], ALU.add, ALU.mult
-            )
-        for u in range(HALVES):
-            nc.vector.tensor_scalar(
-                h_first[u], h_first[u], -2.0, shift_sb[:, first : first + 1], ALU.mult, ALU.add
+                work[1][:, bank_cols(u)], sq_first[u], -0.5, amplitude(0, u)[:], ALU.add, ALU.mult
             )
 
         def put_first_half(u):
+            nc.vector.tensor_scalar(
+                h_first[u], work[1][:, bank_cols(u)], -2.0, shift_sb[:, first : first + 1],
+                ALU.mult, ALU.add,
+            )
             nc.vector.tensor_tensor(
                 page[first][:].indirect(idx2[:, LIST_COLS * u : LIST_COLS * (u + 1)]),
                 h_first[u], wg_first[u][:], ALU.mult,
@@ -256,7 +259,7 @@ def tile_list_slot_trade_table_kernel(
         put_first_half(0)
         for a in range(PASSES):
             nc.vector.quantize_mx(
-                w1_c_rest[a][:].bitcast(FP8X4), w1_s_rest[:, a, :], scratch[a].bitcast(BF16)
+                w1_c_rest[a][:].bitcast(FP8X4), w1_s_rest[:, a, :], w1_bf_rest[a]
             )
         put_first_half(1)
 
@@ -308,7 +311,7 @@ def tile_list_slot_trade_table_kernel(
             nc.vector.tensor_tensor(high[:], morning[:], traded, ALU.max)
             if nxt is not None:
                 nc.vector.tensor_tensor(
-                    page[nxt][:].indirect(idx2[:]), h[:], wg_rest[:, nxt - 1, :], ALU.mult
+                    page[nxt][:].indirect(idx2[:]), h, wg_rest[:, nxt - 1, :], ALU.mult
                 )
             else:
                 nc.vector.quantize_mx(

from contextlib import ExitStack

import concourse.mybir as mybir

K, T, S, H, T2, NPAIR, N = 1024, 2048, 1024, 512, 2048, 512, 384
FLOPS = 2 * 2 * K * H * S + 2 * 2 * H * N * T2

F32 = mybir.dt.float32
BF16 = mybir.dt.bfloat16
I32 = mybir.dt.int32
U32 = mybir.dt.uint32
U16 = mybir.dt.uint16
U8 = mybir.dt.uint8
FP8X4 = mybir.dt.float8_e4m3fn_x4
FP4X4 = mybir.dt.float4_e2m1fn_x4
ALU = mybir.AluOpType
ACT = mybir.ActivationFunctionType

P = 128
PACK = 4
K_PASS = P * PACK
PASSES = K // K_PASS
BANK = 512
HALVES = S // BANK
LIST_COLS = BANK // 16
CHUNKS = T2 // BANK
N_TILES = N // P
QUADS = 4
QUAD = P // QUADS
SCALE_ROWS = 4
REST = PACK - 1
ORDER = (0, 2, 3, 1)
VECTOR_CHUNKS = 2
SHIFT_ROWS = 112


def tile_list_slot_trade_table_kernel(
    tc, tab_words, tab_scales, offs, offs2, offs3, offs4, w1, w2_words, w2_scales,
    shift, wgs, page0, terms, w3, w4_words, w4_scales, out,
):
    nc = tc.nc
    first, last = ORDER[0], ORDER[-1]
    with ExitStack() as ctx:
        keep = ctx.enter_context(tc.tile_pool(name="keep", bufs=1))
        ring = ctx.enter_context(tc.tile_pool(name="ring", bufs=2))
        psum = ctx.enter_context(tc.psum_pool(name="psum", bufs=1))

        def held(shape, dtype, name, tag=None):
            return keep.tile(shape, dtype, name=name, tag=tag or name, align_bytes=64)

        def bank_cols(i):
            return slice(BANK * i, BANK * (i + 1))

        def load_scale_rows(tile, scales):
            for q in range(QUADS):
                rows = scales[:, SCALE_ROWS * q : SCALE_ROWS * (q + 1), :]
                nc.sync.dma_start(
                    tile[QUAD * q : QUAD * q + SCALE_ROWS, :, :].bitcast(I32),
                    rows.rearrange("a r c -> r a c").bitcast(I32),
                )

        idx = held([P, S // 16], U16, "idx")
        idx2 = held([P, S // 16], U16, "idx2")
        idx3 = held([P, NPAIR // 16], U16, "idx3")
        idx4 = held([P, NPAIR // 16], U16, "idx4")

        tab_sc = held([P, T], U8, "tab_sc")
        v_sc = [held([P, S], U8, "v_sc%d" % a) for a in range(PASSES)]
        w2_sc_raw = held([P, PASSES, H], U8, "w2_sc_raw")
        w4_sc = held([P, 1, N], U8, "w4_sc")
        nc.gpsimd.memset(tab_sc[:].bitcast(I32), 0)
        nc.gpsimd.memset(w2_sc_raw[:].rearrange("p a c -> p (a c)").bitcast(I32), 0)
        nc.vector.memset(v_sc[1][:].bitcast(I32), 0)
        nc.vector.memset(w4_sc[:, 0, :].bitcast(I32), 0)

        w2_raw = held([P, PASSES, 2 * H], U8, "w2_raw")
        nc.sync.dma_start(
            w2_raw[:].bitcast(I32), w2_words.rearrange("a p c -> p a c").bitcast(I32)
        )
        for q in range(QUADS):
            nc.sync.dma_start(
                tab_sc[QUAD * q : QUAD * q + PASSES * SCALE_ROWS, :].bitcast(I32),
                tab_scales[:, SCALE_ROWS * q : SCALE_ROWS * (q + 1), :].bitcast(I32),
            )
        nc.sync.dma_start(idx[:], offs)
        tab_w = [held([P, T], U32, "tab_w%d" % a) for a in range(PASSES)]
        for a in range(PASSES):
            nc.sync.dma_start(
                tab_w[a][:].bitcast(I32),
                tab_words[a].rearrange("p t i -> p (t i)").bitcast(I32),
            )
        load_scale_rows(w2_sc_raw, w2_scales)
        w1_raw = [held([P, PACK, H], F32, "w1_raw%d" % a) for a in range(PASSES)]
        for a in range(PASSES):
            nc.sync.dma_start(
                w1_raw[a][:],
                w1[K_PASS * a : K_PASS * (a + 1), :].rearrange("(p j) c -> p j c", j=PACK),
            )
        shift_sb = held([P, PACK], F32, "shift_sb")
        nc.sync.dma_start(shift_sb[:], shift.rearrange("(p t) -> p t", t=PACK))
        nc.sync.dma_start(idx2[:], offs2)

        wgs_rows = wgs.rearrange("(q t) j -> q t j", t=PACK)
        wg_first = [held([P, BANK], F32, "wg_first%d" % u) for u in range(HALVES)]
        wg_rest = held([P, REST, S], F32, "wg_rest")

        def load_wgs(tile, rows):
            for q in range(QUADS):
                nc.sync.dma_start(tile[QUAD * q : QUAD * (q + 1)], rows)

        page = [held([P, T2], F32, "page%d" % t) for t in range(PACK)]
        term = [held([P, NPAIR], F32, "term%d" % t) for t in range(PACK)]
        page_rows = page0.rearrange("(p t) c -> p t c", t=PACK)
        terms_rows = terms.rearrange("(p t) m -> p t m", t=PACK)

        load_wgs(wg_first[0], wgs_rows[:, first, bank_cols(0)])
        nc.sync.dma_start(page[first][:], page_rows[:, first, :])
        load_wgs(wg_first[1], wgs_rows[:, first, bank_cols(1)])
        nc.sync.dma_start(idx4[:], offs4)
        nc.sync.dma_start(idx3[:], offs3)
        nc.sync.dma_start(term[first][:], terms_rows[:, first, :])
        load_wgs(wg_rest, wgs_rows[:, 1:, :])
        for t in ORDER[1:]:
            nc.sync.dma_start(page[t][:], page_rows[:, t, :])
            nc.sync.dma_start(term[t][:], terms_rows[:, t, :])
        w3_raw = held([P, PACK, N], F32, "w3_raw")
        nc.sync.dma_start(w3_raw[:], w3.rearrange("(p j) c -> p j c", j=PACK))
        w4_w = held([P, N], U32, "w4_w")
        nc.sync.dma_start(
            w4_w[:].bitcast(I32), w4_words[0].rearrange("p c i -> p (c i)").bitcast(I32)
        )
        load_scale_rows(w4_sc, w4_scales)

        nc.vector.tensor_copy(v_sc[0][:], tab_sc[:].indirect(idx[:]))
        nc.scalar.dma_start(
            v_sc[1][0:SHIFT_ROWS, :].bitcast(I32),
            v_sc[0][SCALE_ROWS : SCALE_ROWS + SHIFT_ROWS, :].bitcast(I32),
        )
        v_sc_for_w2 = [v_sc[a][:] for a in range(PASSES)]
        v_sc_for_w1 = [v_sc[0][SCALE_ROWS * a :, :] for a in range(PASSES)]

        w2_w = held([P, PASSES, 2 * H], U8, "w2_w")
        w2_sc_cols = w2_sc_raw[:].rearrange("p a (m t) -> p a t m", t=PACK)
        w2_sc_first = held([P, PASSES, P], U8, "w2_sc_first")
        w2_sc_rest = held([P, PASSES, REST, P], U8, "w2_sc_rest")
        for a in range(PASSES):
            nc.gpsimd.tensor_copy(
                w2_w[:, a, :].rearrange("p (t m b) -> p t m b", t=PACK, b=2),
                w2_raw[:, a, :].rearrange("p (m t b) -> p t m b", t=PACK, b=2),
            )
        nc.gpsimd.tensor_copy(w2_sc_first[:], w2_sc_cols[:, :, first, :])
        nc.gpsimd.tensor_copy(w2_sc_rest[:], w2_sc_cols[:, :, 1:, :])

        v_w = [
            [held([P, BANK], U32, "v_w%d_%d" % (a, u)) for u in range(HALVES)]
            for a in range(PASSES)
        ]
        for a in range(PASSES):
            for u in range(HALVES):
                nc.vector.tensor_copy(
                    v_w[a][u][:], tab_w[a][:].indirect(idx[:, LIST_COLS * u : LIST_COLS * (u + 1)])
                )

        w1_cols = [w1_raw[a][:].rearrange("p j (m t) -> p m j t", t=PACK) for a in range(PASSES)]
        w1_c_first = [held([P, P], U32, "w1_c_first%d" % a) for a in range(PASSES)]
        w1_s_first = [held([P, P], U8, "w1_s_first%d" % a) for a in range(PASSES)]
        w1_c_rest = [held([P, REST * P], U32, "w1_c_rest%d" % a) for a in range(PASSES)]
        w1_s_rest = held([P, PASSES, REST * P], U8, "w1_s_rest", tag="wg_first0")
        for a in range(PASSES):
            w1_bf_first = held([P, P, PACK], BF16, "w1_bf_first%d" % a)
            nc.vector.tensor_copy(w1_bf_first[:], w1_cols[a][:, :, :, first])
            nc.vector.quantize_mx(
                w1_c_first[a][:].bitcast(FP8X4), w1_s_first[a][:],
                w1_bf_first[:].rearrange("p m j -> p (m j)"),
            )

        def w1_operand(a, t):
            if t == first:
                return w1_c_first[a][:], w1_s_first[a][:]
            cols = slice(P * (t - 1), P * t)
            return w1_c_rest[a][:, cols], w1_s_rest[:, a, cols]

        def w2_operand(a, t):
            codes = w2_w[:, a, 2 * P * t : 2 * P * (t + 1)]
            return codes, (w2_sc_first[:, a, :] if t == first else w2_sc_rest[:, a, t - 1, :])

        banks = [psum.tile([P, BANK], F32, name="bank%d" % b) for b in range(8)]

        def product(operand, dtype, v_scales, step, u, pair):
            acc = banks[HALVES * (pair % 2) + u]
            for a in range(PASSES):
                codes, scales = operand(a, ORDER[step])
                nc.tensor.matmul_mx(
                    acc[:],
                    lhsT=codes.bitcast(dtype),
                    lhsT_scale=scales,
                    rhs=v_w[a][u][:].bitcast(FP8X4),
                    rhs_scale=v_scales[a][:, bank_cols(u)],
                    start=(a == 0),
                    stop=(a == PASSES - 1),
                )
            return acc

        def sine_squared(step, u, sin_half, sq):
            phase = product(w2_operand, FP4X4, v_sc_for_w2, step, u, step)
            nc.scalar.activation(sin_half, phase[:], ACT.Sin, scale=0.5)
            nc.scalar.activation(sq, sin_half, ACT.Square)

        def amplitude(step, u):
            return product(w1_operand, FP8X4, v_sc_for_w1, step, u, step + 1)

        def factors(step):
            pairs = []
            for u in range(HALVES):
                if (step, u) == (1, 0):
                    sin_half, sq = w1_raw[1][:, 0, :], w1_raw[0][:, 0, :]
                else:
                    sin_half = ring.tile([P, BANK], F32, name="sin_half")[:]
                    sq = ring.tile([P, BANK], F32, name="sq")[:]
                sine_squared(step, u, sin_half, sq)
                cosine = ring.tile([P, BANK], F32, name="cosine", bufs=2 * HALVES)
                nc.scalar.activation(cosine[:], sq, ACT.Identity, bias=1.0, scale=-2.0)
                amp = ring.tile([P, BANK], F32, name="amp", bufs=2 * HALVES)
                nc.scalar.copy(amp[:], amplitude(step, u)[:])
                pairs.append((cosine, amp))
            return pairs

        rest_words = REST * P * PACK // 2
        stage = held([P, PASSES * rest_words], F32, "stage")
        w1_bf_rest = [
            stage[:, rest_words * a : rest_words * (a + 1)].bitcast(BF16) for a in range(PASSES)
        ]
        middle = slice(BANK // 2, BANK // 2 + BANK)
        work = [stage[:, BANK // 2 : BANK // 2 + S], held([P, S], F32, "work1")[:]]
        h_first = [held([P, BANK], F32, "h_lead")[:], work[0][:, middle]]
        sq_first = [ring.tile([P, BANK], F32, name="sq")[:] for u in range(HALVES)]
        for u in range(HALVES):
            sine_squared(0, u, stage[:, bank_cols(u)], sq_first[u])
        for a in range(PASSES):
            nc.scalar.copy(
                w1_bf_rest[a].rearrange("p (t m j) -> p m j t", m=P, j=PACK),
                w1_cols[a][:, :, :, 1:],
            )
        for u in range(HALVES):
            nc.vector.scalar_tensor_tensor(
                work[1][:, bank_cols(u)], sq_first[u], -0.5, amplitude(0, u)[:], ALU.add, ALU.mult
            )

        def put_first_half(u):
            nc.vector.tensor_scalar(
                h_first[u], work[1][:, bank_cols(u)], -2.0, shift_sb[:, first : first + 1],
                ALU.mult, ALU.add,
            )
            nc.vector.tensor_tensor(
                page[first][:].indirect(idx2[:, LIST_COLS * u : LIST_COLS * (u + 1)]),
                h_first[u], wg_first[u][:], ALU.mult,
            )

        put_first_half(0)
        for a in range(PASSES):
            nc.vector.quantize_mx(
                w1_c_rest[a][:].bitcast(FP8X4), w1_s_rest[:, a, :], w1_bf_rest[a]
            )
        put_first_half(1)

        page_bf = [held([P, BANK, PACK], BF16, "page_bf%d" % c) for c in range(CHUNKS)]
        w3_bf = held([P, N, PACK], BF16, "w3_bf")
        w3_c = held([P, N], U32, "w3_c")
        w3_s = held([P, N], U8, "w3_s")

        def round_page(t, c, copy):
            copy(page_bf[c][:, :, t], page[t][:, bank_cols(c)])

        def features(t, pairs, prod, h):
            bias = shift_sb[:, t : t + 1]
            for u, (cosine, amp) in enumerate(pairs):
                nc.gpsimd.tensor_tensor(prod[:, bank_cols(u)], cosine[:], amp[:], ALU.mult)
            for u in range(HALVES):
                cols = bank_cols(u)
                if t == ORDER[1]:
                    nc.scalar.activation(h[:, cols], prod[:, cols], ACT.Identity, bias=bias)
                else:
                    nc.gpsimd.tensor_scalar(h[:, cols], prod[:, cols], 1.0, bias, ALU.mult, ALU.add)

        def put_low(t, low):
            nc.vector.tensor_copy(page[t][:].indirect(idx4[:]), low[:])

        pending = None
        pairs = factors(1)
        for step, t in enumerate(ORDER):
            nxt = ORDER[step + 1] if step < REST else None
            evening = ring.tile([P, NPAIR], F32, name="evening")
            morning = ring.tile([P, NPAIR], F32, name="morning")
            low = ring.tile([P, NPAIR], F32, name="low")
            high = ring.tile([P, NPAIR], F32, name="high")
            prod, h = work[step % 2], work[(step + 1) % 2]
            traded = prod[:, middle]
            if nxt is not None:
                features(nxt, pairs, prod, h)
            nc.vector.tensor_copy(evening[:], page[t][:].indirect(idx4[:]))
            nc.vector.tensor_copy(morning[:], page[t][:].indirect(idx3[:]))
            adder = nc.vector if step == 0 else nc.gpsimd
            adder.tensor_tensor(traded, evening[:], term[t][:], ALU.add)
            if step + 2 < PACK:
                pairs = factors(step + 2)
            if pending is not None:
                put_low(*pending)
                for c in range(CHUNKS):
                    round_page(pending[0], c, nc.scalar.copy)
            nc.vector.tensor_tensor(low[:], morning[:], evening[:], ALU.min)
            nc.vector.tensor_tensor(high[:], morning[:], traded, ALU.max)
            if nxt is not None:
                nc.vector.tensor_tensor(
                    page[nxt][:].indirect(idx2[:]), h, wg_rest[:, nxt - 1, :], ALU.mult
                )
            else:
                nc.vector.quantize_mx(
                    w3_c[:].bitcast(FP8X4), w3_s[:], w3_bf[:].rearrange("p c j -> p (c j)")
                )
            nc.vector.tensor_copy(page[t][:].indirect(idx3[:]), high[:])
            if step == 1:
                nc.scalar.copy(
                    w3_bf[:].rearrange("p (c i) j -> p c j i", i=4),
                    w3_raw[:].rearrange("p j (c i) -> p c j i", i=4),
                )
            pending = (t, low)
        put_low(*pending)

        for c in range(CHUNKS):
            round_page(last, c, nc.vector.tensor_copy if c < VECTOR_CHUNKS else nc.scalar.copy)
        page_c = [held([P, BANK], U32, "page_c%d" % c) for c in range(CHUNKS)]
        page_s = [held([P, BANK], U8, "page_s%d" % c) for c in range(CHUNKS)]
        for c in range(CHUNKS):
            nc.vector.quantize_mx(
                page_c[c][:].bitcast(FP8X4), page_s[c][:],
                page_bf[c][:].rearrange("p c j -> p (c j)"),
            )
        for c in range(CHUNKS):
            for n in range(N_TILES):
                rows = slice(P * n, P * (n + 1))
                turn = (N_TILES * c + n) % 4
                e1, e2 = banks[turn], banks[4 + turn]
                for acc, codes, scales in ((e1, w3_c, w3_s[:]), (e2, w4_w, w4_sc[:, 0, :])):
                    nc.tensor.matmul_mx(
                        acc[:],
                        lhsT=codes[:, rows].bitcast(FP8X4),
                        lhsT_scale=scales[:, rows],
                        rhs=page_c[c][:].bitcast(FP8X4),
                        rhs_scale=page_s[c][:],
                        start=True,
                        stop=True,
                    )
                e1_sb = ring.tile([P, BANK], F32, name="e1_sb", bufs=3)
                nc.scalar.copy(e1_sb[:], e1[:])
                best = ring.tile([P, BANK], F32, name="best", bufs=6)
                nc.vector.tensor_tensor(best[:], e2[:], e1_sb[:], ALU.max)
                nc.sync.dma_start(out[rows, bank_cols(c)], best[:])
